import numpy as np
import ml_dtypes


def mxq(x, axis, fmt="e4m3"):
    dtype, down = {"e4m3": (ml_dtypes.float8_e4m3fn, 7), "e5m2": (ml_dtypes.float8_e5m2, 14)}[fmt]
    v = np.moveaxis(np.asarray(x, np.float32).astype(ml_dtypes.bfloat16).astype(np.float64), axis, -1)
    blocks = v.reshape(v.shape[:-1] + (-1, 32))
    amax = np.abs(blocks).max(-1, keepdims=True)
    byte = np.maximum(np.where(amax > 0, np.frexp(amax)[1] - 1 + 127, 0) - down, 1)
    scale = np.exp2(byte - 127.0)
    codes = (blocks / scale).astype(np.float32).astype(dtype).astype(np.float64)
    return np.moveaxis((codes * scale).reshape(v.shape), -1, axis)


WIDE = False


def mx_kscale(k):
    if not WIDE:
        return np.ones(k)
    levels = np.array([24, -24, 12, -12, 0])
    if k % 512:
        return np.exp2(np.random.permutation(np.resize(levels, k // 32))).repeat(32)
    a = np.empty((k // 512, 16))
    for p in range(k // 512):
        a[p, :8] = np.random.permutation(np.resize(levels, 8))
        for g in range(8):
            far = levels[np.abs(levels - a[p, g]) >= 10]
            a[p, g + 8] = far[np.random.randint(len(far))]
    return np.exp2(a.ravel()).repeat(32)


def f64(x):
    return np.asarray(x).astype(np.float64)


def striped(idx):
    return np.tile(idx.reshape(-1, 16).T, (8, 1)).astype(np.uint16)


def unstriped(offs):
    return offs[:16].T.reshape(-1).astype(np.int64)


E2M1 = np.array([0.0, 0.5, 1.0, 1.5, 2.0, 3.0, 4.0, 6.0, -0.0, -0.5, -1.0, -1.5, -2.0, -3.0, -4.0, -6.0])


def pack_weight(w, fmt):
    k, n = w.shape
    w = f64(np.asarray(w, np.float32).astype(ml_dtypes.bfloat16)).reshape(k // 32, 32, n)
    amax = np.abs(w).max(1)
    if fmt == "e4m3":
        byte = np.frexp(amax)[1] - 1 + 127 - 7
    else:
        mant, ex = np.frexp(amax / 6.0)
        byte = np.where(mant > 0.5, ex, ex - 1) + 127
    byte = np.clip(np.where(amax > 0, byte, 1), 1, 254)
    scaled = (w * np.exp2(127.0 - byte)[:, None, :]).reshape(k, n).astype(np.float32)
    by_word = np.ascontiguousarray(scaled.reshape(k // 512, 128, 4, n).transpose(0, 1, 3, 2))
    if fmt == "e4m3":
        words = by_word.astype(ml_dtypes.float8_e4m3fn).view(np.uint8)
    else:
        c = by_word.astype(ml_dtypes.float4_e2m1fn).view(np.uint8) & 0xF
        words = (c[..., 0::2] | (c[..., 1::2] << 4)).reshape(k // 512, 128, 2 * n)
    return np.ascontiguousarray(words), np.ascontiguousarray(byte.astype(np.uint8).reshape(k // 512, 16, n))


def unpack_weight(words, scales, fmt):
    g, _, n = scales.shape
    words = np.ascontiguousarray(words).reshape(g, 128, n, -1)
    if fmt == "e4m3":
        vals = words.view(ml_dtypes.float8_e4m3fn).astype(np.float64)
    else:
        nib = np.empty((g, 128, n, 4), np.uint8)
        nib[..., 0::2] = words & 0xF
        nib[..., 1::2] = words >> 4
        vals = E2M1[nib]
    vals = vals * np.repeat(np.exp2(scales.astype(np.float64) - 127.0), 8, axis=1)[..., None]
    return vals.transpose(0, 1, 3, 2).reshape(g * 512, n)


def planes(y):
    n, m = y.shape
    v = y.astype(np.float32).astype(ml_dtypes.bfloat16).astype(np.float64).reshape(n // 32, 32, m)
    top = np.abs(v).max(1)
    byte = np.clip(np.where(top > 0, np.frexp(top)[1] - 1 + 127 - 7, 1), 1, 254)
    codes = (v * np.exp2(127.0 - byte)[:, None, :]).reshape(n, m).astype(np.float32).astype(ml_dtypes.float8_e4m3fn).view(np.uint8)
    words = codes.reshape(n // 512, 128, 4, m).transpose(0, 1, 3, 2)
    return np.ascontiguousarray(words), np.ascontiguousarray(byte.astype(np.uint8).reshape(n // 512, 16, m))


def sigm(f):
    return 1.0 / (1.0 + np.exp(-np.maximum(f, -700.0)))


K, M, N, T, J = 1024, 512, 512, 2048, 1024


def setup_inputs():
    n = np.random.standard_normal
    s = mx_kscale(K)[:, None]
    s2 = mx_kscale(M)[:, None]
    h = np.tanh(n((N, T)))
    p_tab = pack_weight(h * s2, "e4m3")
    p_uz = pack_weight(n((M, N)) / np.sqrt(M) / s2, "e4m3")
    p_un = pack_weight(n((M, N)) / np.sqrt(M) / s2, "e4m3")
    return {
        "x": (n((K, J)) * s).astype(np.float32),
        "tab_words": p_tab[0],
        "tab_scales": p_tab[1],
        "wz": (n((K, N)) / np.sqrt(K) / s).astype(np.float32),
        "uz_words": p_uz[0],
        "uz_scales": p_uz[1],
        "wn": (n((K, N)) / np.sqrt(K) / s).astype(np.float32),
        "un_words": p_un[0],
        "un_scales": p_un[1],
        "bz": (0.3 * n(N)).astype(np.float32),
        "bn": (0.3 * n(N)).astype(np.float32),
        "hT": (h).astype(np.float32),
        "wgo": np.tile(np.random.uniform(0.5, 2.0, J), (128, 1)).astype(np.float32),
        "offs": striped(np.random.permutation(T)[:J]),
    }


def reference(x, tab_words, tab_scales, wz, uz_words, uz_scales, wn, un_words, un_scales, bz, bn, hT, wgo, offs):
    idx = unstriped(offs)
    x_ = mxq(f64(x), 0, "e4m3")
    tab_ = unpack_weight(tab_words, tab_scales, "e4m3")[:, idx]
    wz_ = mxq(f64(wz), 0, "e4m3")
    uz_ = unpack_weight(uz_words, uz_scales, "e4m3")
    wn_ = mxq(f64(wn), 0, "e4m3")
    un_ = unpack_weight(un_words, un_scales, "e4m3")
    sz = wz_.T @ x_ + uz_.T @ tab_
    z = sigm(sz + f64(bz)[:, None])
    xn = wn_.T @ x_
    hn = un_.T @ tab_
    cd = np.tanh(xn + f64(bn)[:, None] + z * hn)
    out = np.zeros((N, T))
    out[:, idx] = f64(wgo)[0] * (f64(hT)[:, idx] + z * (cd - f64(hT)[:, idx]))
    return (out,) + planes(out)

@@ -1,0 +1,269 @@
+from contextlib import ExitStack
+
+import concourse.mybir as mybir
+
+K, M, N, T, J = 1024, 512, 512, 2048, 1024
+FLOPS = 2 * J * N * (2 * K + 2 * M)
+
+F32 = mybir.dt.float32
+BF16 = mybir.dt.bfloat16
+I32 = mybir.dt.int32
+U32 = mybir.dt.uint32
+U16 = mybir.dt.uint16
+U8 = mybir.dt.uint8
+FP8X4 = mybir.dt.float8_e4m3fn_x4
+ACT = mybir.ActivationFunctionType
+ALU = mybir.AluOpType
+
+P = 128
+PACK = 4
+K_PASS = P * PACK
+PASSES = K // K_PASS
+HALF = 512
+HALVES = J // HALF
+LIST_COLS = HALF // 16
+CHUNK = 512
+CHUNKS = T // CHUNK
+
+
+def tile_list_tgn_mguP_kernel(
+    tc, x, tab_words, tab_scales, wz, uz_words, uz_scales, wn, un_words, un_scales, bz, bn, hT, wgo, offs,
+    out_0, out_1, out_2,
+):
+    nc = tc.nc
+    with ExitStack() as ctx:
+        keep = ctx.enter_context(tc.tile_pool(name="keep", bufs=1))
+        stage = ctx.enter_context(tc.tile_pool(name="stage", bufs=4))
+        rounded = ctx.enter_context(tc.tile_pool(name="rounded", bufs=3))
+        gates = ctx.enter_context(tc.tile_pool(name="gates", bufs=6))
+        work = ctx.enter_context(tc.tile_pool(name="work", bufs=2))
+        psum3 = ctx.enter_context(tc.psum_pool(name="psum3", bufs=3))
+        psum2 = ctx.enter_context(tc.psum_pool(name="psum2", bufs=2))
+
+        offsets = keep.tile([P, J // 16], U16, name="offsets")
+        nc.sync.dma_start(offsets[:], offs)
+
+        def as_words(ap):
+            return ap[0].rearrange("p c i -> p (c i)").bitcast(I32)
+
+        def zeroed_plane(name, width):
+            plane = keep.tile([P, width], U8, name=name, align_bytes=64)
+            nc.vector.memset(plane[:].bitcast(I32), 0)
+            return plane
+
+        def load_scale_rows(queue, plane, scales):
+            for q in range(4):
+                queue.dma_start(plane[32 * q : 32 * q + 4, :].bitcast(I32), scales[0, 4 * q : 4 * q + 4, :].bitcast(I32))
+
+        uz_plane = zeroed_plane("uz_plane", N)
+        un_plane = zeroed_plane("un_plane", N)
+        tab_plane = zeroed_plane("tab_plane", T)
+        load_scale_rows(nc.gpsimd, uz_plane, uz_scales)
+        load_scale_rows(nc.gpsimd, un_plane, un_scales)
+        bias_z = keep.tile([P, PACK], F32, name="bias_z")
+        bias_n = keep.tile([P, PACK], F32, name="bias_n")
+        nc.gpsimd.dma_start(bias_z[:], bz.rearrange("(p t) -> p t", t=PACK))
+        nc.gpsimd.dma_start(bias_n[:], bn.rearrange("(p t) -> p t", t=PACK))
+
+        tab = keep.tile([P, T], I32, name="tab")
+        nc.sync.dma_start(tab[:], as_words(tab_words))
+        uz_raw = keep.tile([P, N], I32, name="uz_raw")
+        un_raw = keep.tile([P, N], I32, name="un_raw")
+        nc.sync.dma_start(uz_raw[:], as_words(uz_words))
+        nc.sync.dma_start(un_raw[:], as_words(un_words))
+
+        pages = [keep.tile([P, T], F32, name="page%d" % t) for t in range(PACK)]
+        for t in range(PACK):
+            nc.vector.memset(pages[t][:], 0.0)
+
+        def load_rows(src, a, cols):
+            raw = stage.tile([P, PACK, HALF], F32, name="raw")
+            nc.sync.dma_start(raw[:], src[a * K_PASS : (a + 1) * K_PASS, cols].rearrange("(p i) c -> p i c", i=PACK))
+            return raw
+
+        def round_x(copy, raw):
+            grouped = rounded.tile([P, HALF * PACK], BF16, name="grouped", align_bytes=64)
+            copy(
+                grouped[:].rearrange("p (c e i) -> p c i e", e=4, i=PACK),
+                raw[:].rearrange("p i (c e) -> p c i e", e=4),
+            )
+            return grouped
+
+        def round_w(copy, raw):
+            grouped = rounded.tile([P, N * PACK], BF16, name="grouped", align_bytes=64)
+            copy(
+                grouped[:].rearrange("p (t m i) -> p m i t", t=PACK, i=PACK),
+                raw[:].rearrange("p i (m t) -> p m i t", t=PACK),
+            )
+            return grouped
+
+        def quantize(name, grouped):
+            codes = keep.tile([P, HALF], U32, name=name + "_codes", align_bytes=64)
+            plane = keep.tile([P, HALF], U8, name=name + "_plane", align_bytes=64)
+            nc.vector.quantize_mx(out=codes[:].bitcast(FP8X4), scales=plane[:], in_=grouped[:])
+            return codes, plane
+
+        def deal_packed(name, raw, plane):
+            codes = keep.tile([P, N], I32, name=name + "_codes", align_bytes=64)
+            dealt = keep.tile([P, N], U8, name=name + "_dealt", align_bytes=64)
+            nc.vector.tensor_copy(
+                codes[:].rearrange("p (t m) -> p m t", t=PACK), raw[:].rearrange("p (m t) -> p m t", t=PACK)
+            )
+            nc.vector.tensor_copy(
+                dealt[:].rearrange("p (t m) -> p m t", t=PACK), plane[:].rearrange("p (m t) -> p m t", t=PACK)
+            )
+            return codes, dealt
+
+        states = [keep.tile([P, T], F32, name="state%d" % t) for t in range(PACK)]
+        weights = [keep.tile([P, HALF], F32, name="weight%d" % h) for h in range(HALVES)]
+        hT_dealt = hT.rearrange("(p t) c -> t p c", t=PACK)
+        out_dealt = out_0.rearrange("(p t) c -> t p c", t=PACK)
+
+        def half_cols(h):
+            return slice(h * HALF, (h + 1) * HALF)
+
+        def half_list(h):
+            return offsets[:, h * LIST_COLS : (h + 1) * LIST_COLS]
+
+        every = slice(0, N)
+        raw_wz0 = load_rows(wz, 0, every)
+        load_scale_rows(nc.sync, tab_plane, tab_scales)
+        raw_x00 = load_rows(x, 0, half_cols(0))
+        raw_wz1 = load_rows(wz, 1, every)
+
+        v_codes = keep.tile([P, J], U32, name="v_codes", align_bytes=64)
+        v_plane = keep.tile([P, J], U8, name="v_plane", align_bytes=64)
+        nc.vector.tensor_copy(v_codes[:], tab[:].bitcast(U32).indirect(offsets[:]))
+        nc.vector.tensor_copy(v_plane[:], tab_plane[:].indirect(offsets[:]))
+
+        wz_q = [None] * PASSES
+        wn_q = [None] * PASSES
+        x_q = {}
+        wz_q[0] = quantize("wz0", round_w(nc.scalar.copy, raw_wz0))
+        x_q[0, 0] = quantize("x00", round_x(nc.scalar.copy, raw_x00))
+        uz_q = deal_packed("uz", uz_raw, uz_plane)
+        un_q = deal_packed("un", un_raw, un_plane)
+        raw_x10 = load_rows(x, 1, half_cols(0))
+        nc.sync.dma_start(states[0][:], hT_dealt[0])
+        wz_q[1] = quantize("wz1", round_w(nc.scalar.copy, raw_wz1))
+        x_q[1, 0] = quantize("x10", round_x(nc.vector.tensor_copy, raw_x10))
+        raw_wn0 = load_rows(wn, 0, every)
+        raw_wn1 = load_rows(wn, 1, every)
+        nc.sync.dma_start(weights[0][:], wgo[:, half_cols(0)])
+        nc.sync.dma_start(states[1][:], hT_dealt[1])
+        raw_x01 = load_rows(x, 0, half_cols(1))
+        raw_x11 = load_rows(x, 1, half_cols(1))
+        nc.sync.dma_start(weights[1][:], wgo[:, half_cols(1)])
+        nc.sync.dma_start(states[2][:], hT_dealt[2])
+        nc.sync.dma_start(states[3][:], hT_dealt[3])
+
+        def product(acc, t, terms):
+            rows = slice(t * P, (t + 1) * P)
+            for n, (stationary, moving) in enumerate(terms):
+                nc.tensor.matmul_mx(
+                    out=acc[:],
+                    lhsT=stationary[0][:, rows].bitcast(FP8X4),
+                    lhsT_scale=stationary[1][:, rows],
+                    rhs=moving[0].bitcast(FP8X4),
+                    rhs_scale=moving[1],
+                    start=(n == 0),
+                    stop=(n == len(terms) - 1),
+                )
+
+        def x_term(w_q, a, h):
+            return w_q[a], (x_q[a, h][0][:], x_q[a, h][1][:])
+
+        def v_term(u_q, h):
+            return u_q, (v_codes[:, half_cols(h)], v_plane[:, half_cols(h)])
+
+        z, zhn, kept, cand, mixed = {}, {}, {}, {}, {}
+
+        def gate(t, h):
+            sz = psum3.tile([P, HALF], F32, name="sz")
+            hn = psum2.tile([P, HALF], F32, name="hn")
+            product(sz, t, [v_term(uz_q, h)] + [x_term(wz_q, a, h) for a in range(PASSES)])
+            product(hn, t, [v_term(un_q, h)])
+            z[t, h] = gates.tile([P, HALF], F32, name="z")
+            zhn[t, h] = gates.tile([P, HALF], F32, name="zhn")
+            nc.scalar.activation(z[t, h][:], sz[:], ACT.Sigmoid, bias=bias_z[:, t : t + 1])
+            nc.vector.tensor_tensor(zhn[t, h][:], hn[:], z[t, h][:], ALU.mult)
+
+        def keep_state(t, h):
+            rest = work.tile([P, HALF], F32, name="rest")
+            kept[t, h] = work.tile([P, HALF], F32, name="kept")
+            nc.scalar.activation(rest[:], z[t, h][:], ACT.Identity, bias=1.0, scale=-1.0)
+            nc.vector.tensor_tensor(kept[t, h][:], states[t][:].indirect(half_list(h)), rest[:], ALU.mult)
+
+        def candidate(t, h):
+            xn = psum3.tile([P, HALF], F32, name="xn")
+            product(xn, t, [x_term(wn_q, a, h) for a in range(PASSES)])
+            pre = work.tile([P, HALF], F32, name="pre")
+            cand[t, h] = work.tile([P, HALF], F32, name="cand")
+            nc.vector.tensor_tensor(pre[:], xn[:], zhn[t, h][:], ALU.add)
+            nc.scalar.activation(cand[t, h][:], pre[:], ACT.Tanh, bias=bias_n[:, t : t + 1])
+
+        def gate_candidate(t, h):
+            nc.vector.tensor_tensor(cand[t, h][:], cand[t, h][:], z[t, h][:], ALU.mult)
+
+        def mix(t, h):
+            mixed[t, h] = work.tile([P, HALF], F32, name="mixed")
+            nc.vector.tensor_tensor(mixed[t, h][:], cand[t, h][:], kept[t, h][:], ALU.add)
+
+        def scatter(t, h):
+            nc.vector.tensor_tensor(pages[t][:].indirect(half_list(h)), mixed[t, h][:], weights[h][:], ALU.mult)
+
+        y_rounded = [keep.tile([P, CHUNK, PACK], BF16, name="y_rounded%d" % c, align_bytes=64) for c in range(CHUNKS)]
+        y_codes = keep.tile([P, T], U32, name="y_codes", align_bytes=64)
+        y_plane = keep.tile([P, T], U8, name="y_plane", align_bytes=64)
+
+        def round_y(copy, t, c):
+            copy(y_rounded[c][:, :, t], pages[t][:, c * CHUNK : (c + 1) * CHUNK])
+
+        for t in range(PACK):
+            gate(t, 0)
+        wn_q[0] = quantize("wn0", round_w(nc.scalar.copy, raw_wn0))
+        keep_state(0, 0)
+        wn_q[1] = quantize("wn1", round_w(nc.vector.tensor_copy, raw_wn1))
+
+        steps = [(0, 0), (1, 0), (0, 1), (1, 1), (2, 0), (2, 1), (3, 0), (3, 1)]
+        candidate(*steps[0])
+        x_round = [round_x(nc.scalar.copy, raw_x01), round_x(nc.scalar.copy, raw_x11)]
+        pending = []
+        for s, (t, h) in enumerate(steps):
+            following = steps[s + 1] if s + 1 < len(steps) else None
+            gate_candidate(t, h)
+            if following and following not in z:
+                gate(*following)
+            mix(t, h)
+            if following:
+                candidate(*following)
+            scatter(t, h)
+            if s == 0:
+                for a in range(PASSES):
+                    x_q[a, 1] = quantize("x%d1" % a, x_round[a])
+            if following:
+                keep_state(*following)
+            for job in pending[:3]:
+                round_y(nc.scalar.copy, *job)
+            pending = pending[3:]
+            if h == HALVES - 1:
+                nc.sync.dma_start(out_dealt[t], pages[t][:])
+                if t < PACK - 1:
+                    pending = pending + [(t, c) for c in range(CHUNKS)]
+        for job in pending:
+            round_y(nc.scalar.copy, *job)
+
+        last = PACK - 1
+        words_out = as_words(out_1)
+        for c in range(CHUNKS):
+            round_y(nc.vector.tensor_copy if c < CHUNKS // 2 else nc.scalar.copy, last, c)
+        for c in range(CHUNKS):
+            cols = slice(c * CHUNK, (c + 1) * CHUNK)
+            nc.vector.quantize_mx(
+                out=y_codes[:, cols].bitcast(FP8X4),
+                scales=y_plane[:, cols],
+                in_=y_rounded[c][:].rearrange("p c i -> p (c i)"),
+            )
+            nc.sync.dma_start(words_out[:, cols], y_codes[:, cols].bitcast(I32))
+        for q in range(4):
+            nc.scalar.dma_start(out_2[0, 4 * q : 4 * q + 4, :].bitcast(I32), y_plane[32 * q : 32 * q + 4, :].bitcast(I32))

@@ -34,8 +34,8 @@ def tile_list_tgn_mguP_kernel(
     with ExitStack() as ctx:
         keep = ctx.enter_context(tc.tile_pool(name="keep", bufs=1))
         stage = ctx.enter_context(tc.tile_pool(name="stage", bufs=4))
-        rounded = ctx.enter_context(tc.tile_pool(name="rounded", bufs=3))
-        gates = ctx.enter_context(tc.tile_pool(name="gates", bufs=6))
+        rounded = ctx.enter_context(tc.tile_pool(name="rounded", bufs=2))
+        gates = ctx.enter_context(tc.tile_pool(name="gates", bufs=8))
         work = ctx.enter_context(tc.tile_pool(name="work", bufs=2))
         psum3 = ctx.enter_context(tc.psum_pool(name="psum3", bufs=3))
         psum2 = ctx.enter_context(tc.psum_pool(name="psum2", bufs=2))
@@ -51,26 +51,19 @@ def tile_list_tgn_mguP_kernel(
             nc.vector.memset(plane[:].bitcast(I32), 0)
             return plane
 
-        def load_scale_rows(queue, plane, scales):
+        def load_scale_rows(plane, first, scales):
             for q in range(4):
-                queue.dma_start(plane[32 * q : 32 * q + 4, :].bitcast(I32), scales[0, 4 * q : 4 * q + 4, :].bitcast(I32))
+                rows = slice(32 * q + first, 32 * q + first + 4)
+                nc.sync.dma_start(plane[rows, :].bitcast(I32), scales[0, 4 * q : 4 * q + 4, :].bitcast(I32))
 
-        uz_plane = zeroed_plane("uz_plane", N)
-        un_plane = zeroed_plane("un_plane", N)
         tab_plane = zeroed_plane("tab_plane", T)
-        load_scale_rows(nc.gpsimd, uz_plane, uz_scales)
-        load_scale_rows(nc.gpsimd, un_plane, un_scales)
+        u_plane = zeroed_plane("u_plane", N)
         bias_z = keep.tile([P, PACK], F32, name="bias_z")
         bias_n = keep.tile([P, PACK], F32, name="bias_n")
-        nc.gpsimd.dma_start(bias_z[:], bz.rearrange("(p t) -> p t", t=PACK))
-        nc.gpsimd.dma_start(bias_n[:], bn.rearrange("(p t) -> p t", t=PACK))
-
         tab = keep.tile([P, T], I32, name="tab")
-        nc.sync.dma_start(tab[:], as_words(tab_words))
         uz_raw = keep.tile([P, N], I32, name="uz_raw")
         un_raw = keep.tile([P, N], I32, name="un_raw")
-        nc.sync.dma_start(uz_raw[:], as_words(uz_words))
-        nc.sync.dma_start(un_raw[:], as_words(un_words))
+        nc.sync.dma_start(tab[:], as_words(tab_words))
 
         pages = [keep.tile([P, T], F32, name="page%d" % t) for t in range(PACK)]
         for t in range(PACK):
@@ -103,16 +96,12 @@ def tile_list_tgn_mguP_kernel(
             nc.vector.quantize_mx(out=codes[:].bitcast(FP8X4), scales=plane[:], in_=grouped[:])
             return codes, plane
 
-        def deal_packed(name, raw, plane):
-            codes = keep.tile([P, N], I32, name=name + "_codes", align_bytes=64)
-            dealt = keep.tile([P, N], U8, name=name + "_dealt", align_bytes=64)
+        def deal_packed(name, raw, dtype):
+            dealt = keep.tile([P, N], dtype, name=name, align_bytes=64)
             nc.vector.tensor_copy(
-                codes[:].rearrange("p (t m) -> p m t", t=PACK), raw[:].rearrange("p (m t) -> p m t", t=PACK)
+                dealt[:].rearrange("p (t m) -> p m t", t=PACK), raw[:].rearrange("p (m t) -> p m t", t=PACK)
             )
-            nc.vector.tensor_copy(
-                dealt[:].rearrange("p (t m) -> p m t", t=PACK), plane[:].rearrange("p (m t) -> p m t", t=PACK)
-            )
-            return codes, dealt
+            return dealt
 
         states = [keep.tile([P, T], F32, name="state%d" % t) for t in range(PACK)]
         weights = [keep.tile([P, HALF], F32, name="weight%d" % h) for h in range(HALVES)]
@@ -127,9 +116,16 @@ def tile_list_tgn_mguP_kernel(
 
         every = slice(0, N)
         raw_wz0 = load_rows(wz, 0, every)
-        load_scale_rows(nc.sync, tab_plane, tab_scales)
+        load_scale_rows(tab_plane, 0, tab_scales)
         raw_x00 = load_rows(x, 0, half_cols(0))
+        nc.sync.dma_start(uz_raw[:], as_words(uz_words))
         raw_wz1 = load_rows(wz, 1, every)
+        load_scale_rows(u_plane, 0, uz_scales)
+        nc.sync.dma_start(un_raw[:], as_words(un_words))
+        raw_x10 = load_rows(x, 1, half_cols(0))
+        load_scale_rows(u_plane, 4, un_scales)
+        nc.sync.dma_start(bias_z[:], bz.rearrange("(p t) -> p t", t=PACK))
+        nc.sync.dma_start(states[0][:], hT_dealt[0])
 
         v_codes = keep.tile([P, J], U32, name="v_codes", align_bytes=64)
         v_plane = keep.tile([P, J], U8, name="v_plane", align_bytes=64)
@@ -141,14 +137,16 @@ def tile_list_tgn_mguP_kernel(
         x_q = {}
         wz_q[0] = quantize("wz0", round_w(nc.scalar.copy, raw_wz0))
         x_q[0, 0] = quantize("x00", round_x(nc.scalar.copy, raw_x00))
-        uz_q = deal_packed("uz", uz_raw, uz_plane)
-        un_q = deal_packed("un", un_raw, un_plane)
-        raw_x10 = load_rows(x, 1, half_cols(0))
-        nc.sync.dma_start(states[0][:], hT_dealt[0])
+        uz_codes = deal_packed("uz_codes", uz_raw, I32)
+        un_codes = deal_packed("un_codes", un_raw, I32)
         wz_q[1] = quantize("wz1", round_w(nc.scalar.copy, raw_wz1))
         x_q[1, 0] = quantize("x10", round_x(nc.vector.tensor_copy, raw_x10))
+        u_dealt = deal_packed("u_dealt", u_plane, U8)
+        uz_q = uz_codes, u_dealt[:]
+        un_q = un_codes, u_dealt[4:P, :]
         raw_wn0 = load_rows(wn, 0, every)
         raw_wn1 = load_rows(wn, 1, every)
+        nc.sync.dma_start(bias_n[:], bn.rearrange("(p t) -> p t", t=PACK))
         nc.sync.dma_start(weights[0][:], wgo[:, half_cols(0)])
         nc.sync.dma_start(states[1][:], hT_dealt[1])
         raw_x01 = load_rows(x, 0, half_cols(1))
@@ -176,7 +174,7 @@ def tile_list_tgn_mguP_kernel(
         def v_term(u_q, h):
             return u_q, (v_codes[:, half_cols(h)], v_plane[:, half_cols(h)])
 
-        z, zhn, kept, cand, mixed = {}, {}, {}, {}, {}
+        z, zhn, kept, cand = {}, {}, {}, {}
 
         def gate(t, h):
             sz = psum3.tile([P, HALF], F32, name="sz")
@@ -190,34 +188,36 @@ def tile_list_tgn_mguP_kernel(
 
         def keep_state(t, h):
             rest = work.tile([P, HALF], F32, name="rest")
-            kept[t, h] = work.tile([P, HALF], F32, name="kept")
+            kept[t, h] = gates.tile([P, HALF], F32, name="kept")
             nc.scalar.activation(rest[:], z[t, h][:], ACT.Identity, bias=1.0, scale=-1.0)
-            nc.vector.tensor_tensor(kept[t, h][:], states[t][:].indirect(half_list(h)), rest[:], ALU.mult)
+            nc.vector.tensor_copy(kept[t, h][:], states[t][:].indirect(half_list(h)))
+            nc.gpsimd.tensor_tensor(kept[t, h][:], kept[t, h][:], rest[:], ALU.mult)
 
         def candidate(t, h):
             xn = psum3.tile([P, HALF], F32, name="xn")
             product(xn, t, [x_term(wn_q, a, h) for a in range(PASSES)])
-            pre = work.tile([P, HALF], F32, name="pre")
-            cand[t, h] = work.tile([P, HALF], F32, name="cand")
-            nc.vector.tensor_tensor(pre[:], xn[:], zhn[t, h][:], ALU.add)
-            nc.scalar.activation(cand[t, h][:], pre[:], ACT.Tanh, bias=bias_n[:, t : t + 1])
+            cand[t, h] = zhn[t, h]
+            nc.vector.tensor_tensor(cand[t, h][:], xn[:], zhn[t, h][:], ALU.add)
+            nc.scalar.activation(cand[t, h][:], cand[t, h][:], ACT.Tanh, bias=bias_n[:, t : t + 1])
 
-        def gate_candidate(t, h):
-            nc.vector.tensor_tensor(cand[t, h][:], cand[t, h][:], z[t, h][:], ALU.mult)
-
-        def mix(t, h):
-            mixed[t, h] = work.tile([P, HALF], F32, name="mixed")
-            nc.vector.tensor_tensor(mixed[t, h][:], cand[t, h][:], kept[t, h][:], ALU.add)
+        def blend(t, h):
+            new = cand[t, h][:]
+            nc.gpsimd.tensor_tensor(new, new, z[t, h][:], ALU.mult)
+            nc.gpsimd.tensor_tensor(new, new, kept[t, h][:], ALU.add)
+            nc.gpsimd.tensor_tensor(new, new, weights[h][:], ALU.mult)
 
         def scatter(t, h):
-            nc.vector.tensor_tensor(pages[t][:].indirect(half_list(h)), mixed[t, h][:], weights[h][:], ALU.mult)
+            nc.vector.tensor_copy(pages[t][:].indirect(half_list(h)), cand[t, h][:])
 
         y_rounded = [keep.tile([P, CHUNK, PACK], BF16, name="y_rounded%d" % c, align_bytes=64) for c in range(CHUNKS)]
         y_codes = keep.tile([P, T], U32, name="y_codes", align_bytes=64)
         y_plane = keep.tile([P, T], U8, name="y_plane", align_bytes=64)
 
+        upper = [keep.tile([P, 2, CHUNK], BF16, name="upper%d" % c) for c in range(CHUNKS // 2)]
+
         def round_y(copy, t, c):
-            copy(y_rounded[c][:, :, t], pages[t][:, c * CHUNK : (c + 1) * CHUNK])
+            by_rows = t >= 2 and c < CHUNKS // 2
+            copy(upper[c][:, t - 2, :] if by_rows else y_rounded[c][:, :, t], pages[t][:, c * CHUNK : (c + 1) * CHUNK])
 
         for t in range(PACK):
             gate(t, 0)
@@ -228,21 +228,22 @@ def tile_list_tgn_mguP_kernel(
         steps = [(0, 0), (1, 0), (0, 1), (1, 1), (2, 0), (2, 1), (3, 0), (3, 1)]
         candidate(*steps[0])
         x_round = [round_x(nc.scalar.copy, raw_x01), round_x(nc.scalar.copy, raw_x11)]
+        blend(*steps[0])
+        candidate(*steps[1])
+        keep_state(*steps[1])
+        for a in range(PASSES):
+            x_q[a, 1] = quantize("x%d1" % a, x_round[a])
         pending = []
         for s, (t, h) in enumerate(steps):
-            following = steps[s + 1] if s + 1 < len(steps) else None
-            gate_candidate(t, h)
-            if following and following not in z:
-                gate(*following)
-            mix(t, h)
-            if following:
-                candidate(*following)
+            if s + 1 < len(steps):
+                blend(*steps[s + 1])
+            if s + 2 < len(steps):
+                ahead = steps[s + 2]
+                if ahead not in z:
+                    gate(*ahead)
+                keep_state(*ahead)
+                candidate(*ahead)
             scatter(t, h)
-            if s == 0:
-                for a in range(PASSES):
-                    x_q[a, 1] = quantize("x%d1" % a, x_round[a])
-            if following:
-                keep_state(*following)
             for job in pending[:3]:
                 round_y(nc.scalar.copy, *job)
             pending = pending[3:]
@@ -257,6 +258,8 @@ def tile_list_tgn_mguP_kernel(
         words_out = as_words(out_1)
         for c in range(CHUNKS):
             round_y(nc.vector.tensor_copy if c < CHUNKS // 2 else nc.scalar.copy, last, c)
+        for c in range(CHUNKS // 2):
+            nc.vector.tensor_copy(y_rounded[c][:, :, 2:4], upper[c][:].rearrange("p i c -> p c i"))
         for c in range(CHUNKS):
             cols = slice(c * CHUNK, (c + 1) * CHUNK)
             nc.vector.quantize_mx(

@@ -1,6 +1,7 @@
 from contextlib import ExitStack
 
 import concourse.mybir as mybir
+from concourse.masks import make_identity
 
 K, M, N, T, J = 1024, 512, 512, 2048, 1024
 FLOPS = 2 * J * N * (2 * K + 2 * M)
@@ -33,12 +34,11 @@ def tile_list_tgn_mguP_kernel(
     nc = tc.nc
     with ExitStack() as ctx:
         keep = ctx.enter_context(tc.tile_pool(name="keep", bufs=1))
-        stage = ctx.enter_context(tc.tile_pool(name="stage", bufs=4))
-        rounded = ctx.enter_context(tc.tile_pool(name="rounded", bufs=2))
-        gates = ctx.enter_context(tc.tile_pool(name="gates", bufs=8))
+        stage = ctx.enter_context(tc.tile_pool(name="stage", bufs=8))
+        rounded = ctx.enter_context(tc.tile_pool(name="rounded", bufs=3))
+        gates = ctx.enter_context(tc.tile_pool(name="gates", bufs=4))
         work = ctx.enter_context(tc.tile_pool(name="work", bufs=2))
-        psum3 = ctx.enter_context(tc.psum_pool(name="psum3", bufs=3))
-        psum2 = ctx.enter_context(tc.psum_pool(name="psum2", bufs=2))
+        psum = ctx.enter_context(tc.psum_pool(name="psum", bufs=1))
 
         offsets = keep.tile([P, J // 16], U16, name="offsets")
         nc.sync.dma_start(offsets[:], offs)
@@ -48,7 +48,7 @@ def tile_list_tgn_mguP_kernel(
 
         def zeroed_plane(name, width):
             plane = keep.tile([P, width], U8, name=name, align_bytes=64)
-            nc.vector.memset(plane[:].bitcast(I32), 0)
+            nc.gpsimd.memset(plane[:].bitcast(I32), 0)
             return plane
 
         def load_scale_rows(plane, first, scales):
@@ -60,40 +60,42 @@ def tile_list_tgn_mguP_kernel(
         u_plane = zeroed_plane("u_plane", N)
         bias_z = keep.tile([P, PACK], F32, name="bias_z")
         bias_n = keep.tile([P, PACK], F32, name="bias_n")
-        tab = keep.tile([P, T], I32, name="tab")
+        tab = stage.tile([P, T], I32, name="raw")
         uz_raw = keep.tile([P, N], I32, name="uz_raw")
         un_raw = keep.tile([P, N], I32, name="un_raw")
         nc.sync.dma_start(tab[:], as_words(tab_words))
 
         pages = [keep.tile([P, T], F32, name="page%d" % t) for t in range(PACK)]
         for t in range(PACK):
-            nc.vector.memset(pages[t][:], 0.0)
+            nc.gpsimd.memset(pages[t][:], 0.0)
 
         def load_rows(src, a, cols):
             raw = stage.tile([P, PACK, HALF], F32, name="raw")
             nc.sync.dma_start(raw[:], src[a * K_PASS : (a + 1) * K_PASS, cols].rearrange("(p i) c -> p i c", i=PACK))
             return raw
 
-        def round_x(copy, raw):
+        def round_x(raw, parts):
             grouped = rounded.tile([P, HALF * PACK], BF16, name="grouped", align_bytes=64)
-            copy(
-                grouped[:].rearrange("p (c e i) -> p c i e", e=4, i=PACK),
-                raw[:].rearrange("p i (c e) -> p c i e", e=4),
-            )
-            return grouped
+            for copy, first, stop in parts:
+                copy(
+                    grouped[:, first * PACK : stop * PACK].rearrange("p (c e i) -> p c i e", e=4, i=PACK),
+                    raw[:, :, first:stop].rearrange("p i (c e) -> p c i e", e=4),
+                )
+            return grouped[:]
 
-        def round_w(copy, raw):
-            grouped = rounded.tile([P, N * PACK], BF16, name="grouped", align_bytes=64)
-            copy(
-                grouped[:].rearrange("p (t m i) -> p m i t", t=PACK, i=PACK),
-                raw[:].rearrange("p i (m t) -> p m i t", t=PACK),
-            )
-            return grouped
+        def round_w(raw, parts):
+            grouped = rounded.tile([P, PACK, P * PACK], BF16, name="grouped", align_bytes=64)
+            for copy, first, stop in parts:
+                copy(
+                    grouped[:, first:stop, :].rearrange("p t (m i) -> p m i t", i=PACK),
+                    raw[:].rearrange("p i (m t) -> p m i t", t=PACK)[:, :, :, first:stop],
+                )
+            return grouped[:].rearrange("p t c -> p (t c)")
 
         def quantize(name, grouped):
             codes = keep.tile([P, HALF], U32, name=name + "_codes", align_bytes=64)
             plane = keep.tile([P, HALF], U8, name=name + "_plane", align_bytes=64)
-            nc.vector.quantize_mx(out=codes[:].bitcast(FP8X4), scales=plane[:], in_=grouped[:])
+            nc.vector.quantize_mx(out=codes[:].bitcast(FP8X4), scales=plane[:], in_=grouped)
             return codes, plane
 
         def deal_packed(name, raw, dtype):
@@ -103,30 +105,44 @@ def tile_list_tgn_mguP_kernel(
             )
             return dealt
 
-        states = [keep.tile([P, T], F32, name="state%d" % t) for t in range(PACK)]
-        weights = [keep.tile([P, HALF], F32, name="weight%d" % h) for h in range(HALVES)]
+        states = [None] * PACK
+        weights = keep.tile([P, J], F32, name="weights")
         hT_dealt = hT.rearrange("(p t) c -> t p c", t=PACK)
         out_dealt = out_0.rearrange("(p t) c -> t p c", t=PACK)
+        identity = keep.tile([P, P], F32, name="identity")
+        make_identity(nc, identity[:])
+
+        def load_state(t):
+            states[t] = stage.tile([P, T], F32, name="raw")
+            nc.sync.dma_start(states[t][:], hT_dealt[t])
 
         def half_cols(h):
             return slice(h * HALF, (h + 1) * HALF)
 
-        def half_list(h):
-            return offsets[:, h * LIST_COLS : (h + 1) * LIST_COLS]
-
         every = slice(0, N)
-        raw_wz0 = load_rows(wz, 0, every)
         load_scale_rows(tab_plane, 0, tab_scales)
+        raw_wz0 = load_rows(wz, 0, every)
         raw_x00 = load_rows(x, 0, half_cols(0))
         nc.sync.dma_start(uz_raw[:], as_words(uz_words))
-        raw_wz1 = load_rows(wz, 1, every)
         load_scale_rows(u_plane, 0, uz_scales)
+        raw_wz1 = load_rows(wz, 1, every)
         nc.sync.dma_start(un_raw[:], as_words(un_words))
         raw_x10 = load_rows(x, 1, half_cols(0))
         load_scale_rows(u_plane, 4, un_scales)
         nc.sync.dma_start(bias_z[:], bz.rearrange("(p t) -> p t", t=PACK))
-        nc.sync.dma_start(states[0][:], hT_dealt[0])
+        raw_x01 = load_rows(x, 0, half_cols(1))
+        raw_x11 = load_rows(x, 1, half_cols(1))
+        raw_wn0 = load_rows(wn, 0, every)
+        load_state(0)
+        raw_wn1 = load_rows(wn, 1, every)
+        nc.sync.dma_start(bias_n[:], bn.rearrange("(p t) -> p t", t=PACK))
+        load_state(1)
+        nc.sync.dma_start(weights[:, half_cols(0)], wgo[:, half_cols(0)])
+        nc.sync.dma_start(weights[:, half_cols(1)], wgo[:, half_cols(1)])
+        load_state(2)
+        load_state(3)
 
+        on_scalar, on_vector = nc.scalar.copy, nc.vector.tensor_copy
         v_codes = keep.tile([P, J], U32, name="v_codes", align_bytes=64)
         v_plane = keep.tile([P, J], U8, name="v_plane", align_bytes=64)
         nc.vector.tensor_copy(v_codes[:], tab[:].bitcast(U32).indirect(offsets[:]))
@@ -135,25 +151,15 @@ def tile_list_tgn_mguP_kernel(
         wz_q = [None] * PASSES
         wn_q = [None] * PASSES
         x_q = {}
-        wz_q[0] = quantize("wz0", round_w(nc.scalar.copy, raw_wz0))
-        x_q[0, 0] = quantize("x00", round_x(nc.scalar.copy, raw_x00))
+        wz_q[0] = quantize("wz0", round_w(raw_wz0, [(on_scalar, 0, 4)]))
+        x_q[0, 0] = quantize("x00", round_x(raw_x00, [(on_scalar, 0, HALF)]))
         uz_codes = deal_packed("uz_codes", uz_raw, I32)
         un_codes = deal_packed("un_codes", un_raw, I32)
-        wz_q[1] = quantize("wz1", round_w(nc.scalar.copy, raw_wz1))
-        x_q[1, 0] = quantize("x10", round_x(nc.vector.tensor_copy, raw_x10))
         u_dealt = deal_packed("u_dealt", u_plane, U8)
         uz_q = uz_codes, u_dealt[:]
         un_q = un_codes, u_dealt[4:P, :]
-        raw_wn0 = load_rows(wn, 0, every)
-        raw_wn1 = load_rows(wn, 1, every)
-        nc.sync.dma_start(bias_n[:], bn.rearrange("(p t) -> p t", t=PACK))
-        nc.sync.dma_start(weights[0][:], wgo[:, half_cols(0)])
-        nc.sync.dma_start(states[1][:], hT_dealt[1])
-        raw_x01 = load_rows(x, 0, half_cols(1))
-        raw_x11 = load_rows(x, 1, half_cols(1))
-        nc.sync.dma_start(weights[1][:], wgo[:, half_cols(1)])
-        nc.sync.dma_start(states[2][:], hT_dealt[2])
-        nc.sync.dma_start(states[3][:], hT_dealt[3])
+        wz_q[1] = quantize("wz1", round_w(raw_wz1, [(on_scalar, 0, 2), (on_vector, 2, 4)]))
+        x_q[1, 0] = quantize("x10", round_x(raw_x10, [(on_scalar, 0, 192), (on_vector, 192, HALF)]))
 
         def product(acc, t, terms):
             rows = slice(t * P, (t + 1) * P)
@@ -174,85 +180,109 @@ def tile_list_tgn_mguP_kernel(
         def v_term(u_q, h):
             return u_q, (v_codes[:, half_cols(h)], v_plane[:, half_cols(h)])
 
-        z, zhn, kept, cand = {}, {}, {}, {}
+        z = [gates.tile([P, J], F32, name="z") for t in range(PACK)]
+        zhn = [gates.tile([P, J], F32, name="zhn") for t in range(PACK)]
+        scratch = [keep.tile([P, CHUNK * PACK // 2], F32, name="scratch%d" % c, align_bytes=64) for c in range(CHUNKS)]
+        kept = {}
+
+        def span(halves):
+            return slice(halves[0] * HALF, (halves[-1] + 1) * HALF)
+
+        def listed(halves):
+            return offsets[:, halves[0] * LIST_COLS : (halves[-1] + 1) * LIST_COLS]
 
         def gate(t, h):
-            sz = psum3.tile([P, HALF], F32, name="sz")
-            hn = psum2.tile([P, HALF], F32, name="hn")
+            sz = psum.tile([P, HALF], F32, name="sz", tag="a", bufs=3)
+            hn = psum.tile([P, HALF], F32, name="hn", tag="b", bufs=2)
             product(sz, t, [v_term(uz_q, h)] + [x_term(wz_q, a, h) for a in range(PASSES)])
             product(hn, t, [v_term(un_q, h)])
-            z[t, h] = gates.tile([P, HALF], F32, name="z")
-            zhn[t, h] = gates.tile([P, HALF], F32, name="zhn")
-            nc.scalar.activation(z[t, h][:], sz[:], ACT.Sigmoid, bias=bias_z[:, t : t + 1])
-            nc.vector.tensor_tensor(zhn[t, h][:], hn[:], z[t, h][:], ALU.mult)
+            nc.scalar.activation(z[t][:, half_cols(h)], sz[:], ACT.Sigmoid, bias=bias_z[:, t : t + 1])
+            nc.vector.tensor_tensor(zhn[t][:, half_cols(h)], hn[:], z[t][:, half_cols(h)], ALU.mult)
 
-        def keep_state(t, h):
-            rest = work.tile([P, HALF], F32, name="rest")
-            kept[t, h] = gates.tile([P, HALF], F32, name="kept")
-            nc.scalar.activation(rest[:], z[t, h][:], ACT.Identity, bias=1.0, scale=-1.0)
-            nc.vector.tensor_copy(kept[t, h][:], states[t][:].indirect(half_list(h)))
-            nc.gpsimd.tensor_tensor(kept[t, h][:], kept[t, h][:], rest[:], ALU.mult)
+        def keep_state(t, halves):
+            width = HALF * len(halves)
+            rest = work.tile([P, width], F32, name="rest", bufs=2)
+            kept[t, halves] = work.tile([P, width], F32, name="kept", bufs=4)
+            nc.scalar.activation(rest[:], z[t][:, span(halves)], ACT.Identity, bias=1.0, scale=-1.0)
+            nc.vector.tensor_tensor(kept[t, halves][:], states[t][:].indirect(listed(halves)), rest[:], ALU.mult)
 
         def candidate(t, h):
-            xn = psum3.tile([P, HALF], F32, name="xn")
+            xn = psum.tile([P, HALF], F32, name="xn", tag="a", bufs=3)
             product(xn, t, [x_term(wn_q, a, h) for a in range(PASSES)])
-            cand[t, h] = zhn[t, h]
-            nc.vector.tensor_tensor(cand[t, h][:], xn[:], zhn[t, h][:], ALU.add)
-            nc.scalar.activation(cand[t, h][:], cand[t, h][:], ACT.Tanh, bias=bias_n[:, t : t + 1])
+            biased = [scratch[b][:, h * P : (h + 1) * P] for b in range(HALF // P)]
+            for b in range(HALF // P):
+                nc.scalar.activation(biased[b], xn[:, b * P : (b + 1) * P], ACT.Identity, bias=bias_n[:, t : t + 1])
+            pre = psum.tile([P, HALF], F32, name="pre", tag="b", bufs=2)
+            for b in range(HALF // P):
+                block = slice(b * P, (b + 1) * P)
+                events = slice(h * HALF + b * P, h * HALF + (b + 1) * P)
+                nc.tensor.matmul(pre[:, block], biased[b], identity[:], is_transpose=True, start=True, stop=False)
+                nc.tensor.matmul(pre[:, block], zhn[t][:, events], identity[:], is_transpose=True, start=False, stop=True)
+            nc.scalar.activation(zhn[t][:, half_cols(h)], pre[:], ACT.Tanh)
 
-        def blend(t, h):
-            new = cand[t, h][:]
-            nc.gpsimd.tensor_tensor(new, new, z[t, h][:], ALU.mult)
-            nc.gpsimd.tensor_tensor(new, new, kept[t, h][:], ALU.add)
-            nc.gpsimd.tensor_tensor(new, new, weights[h][:], ALU.mult)
+        def first_candidate(t, h):
+            xn = psum.tile([P, HALF], F32, name="xn", tag="a", bufs=3)
+            product(xn, t, [x_term(wn_q, a, h) for a in range(PASSES)])
+            part = zhn[t][:, half_cols(h)]
+            nc.vector.tensor_tensor(part, xn[:], part, ALU.add)
+            nc.scalar.activation(part, part, ACT.Tanh, bias=bias_n[:, t : t + 1])
+            nc.vector.tensor_tensor(part, part, z[t][:, half_cols(h)], ALU.mult)
 
-        def scatter(t, h):
-            nc.vector.tensor_copy(pages[t][:].indirect(half_list(h)), cand[t, h][:])
+        def gate_candidate(t, halves):
+            for h in halves:
+                cand = psum.tile([P, HALF], F32, name="cand", tag="c", bufs=3)
+                for b in range(HALF // P):
+                    events = slice(h * HALF + b * P, h * HALF + (b + 1) * P)
+                    nc.tensor.transpose(cand[:, b * P : (b + 1) * P], zhn[t][:, events], identity[:])
+                nc.vector.tensor_tensor(zhn[t][:, half_cols(h)], cand[:], z[t][:, half_cols(h)], ALU.mult)
 
-        y_rounded = [keep.tile([P, CHUNK, PACK], BF16, name="y_rounded%d" % c, align_bytes=64) for c in range(CHUNKS)]
+        def mix(t, halves):
+            part = zhn[t][:, span(halves)]
+            nc.vector.tensor_tensor(part, part, kept[t, halves][:], ALU.add)
+
+        def scatter(t, halves):
+            nc.vector.tensor_tensor(
+                pages[t][:].indirect(listed(halves)), zhn[t][:, span(halves)], weights[:, span(halves)], ALU.mult
+            )
+
+        y_rounded = [scratch[c][:].bitcast(BF16).rearrange("p (c i) -> p c i", i=PACK) for c in range(CHUNKS)]
         y_codes = keep.tile([P, T], U32, name="y_codes", align_bytes=64)
         y_plane = keep.tile([P, T], U8, name="y_plane", align_bytes=64)
-
         upper = [keep.tile([P, 2, CHUNK], BF16, name="upper%d" % c) for c in range(CHUNKS // 2)]
 
         def round_y(copy, t, c):
             by_rows = t >= 2 and c < CHUNKS // 2
             copy(upper[c][:, t - 2, :] if by_rows else y_rounded[c][:, :, t], pages[t][:, c * CHUNK : (c + 1) * CHUNK])
 
+        both = (0, 1)
+        steps = [(t, both) for t in range(PACK)]
+        on_vector_alone = ((0, 0), (0, 1))
         for t in range(PACK):
             gate(t, 0)
-        wn_q[0] = quantize("wn0", round_w(nc.scalar.copy, raw_wn0))
-        keep_state(0, 0)
-        wn_q[1] = quantize("wn1", round_w(nc.vector.tensor_copy, raw_wn1))
-
-        steps = [(0, 0), (1, 0), (0, 1), (1, 1), (2, 0), (2, 1), (3, 0), (3, 1)]
-        candidate(*steps[0])
-        x_round = [round_x(nc.scalar.copy, raw_x01), round_x(nc.scalar.copy, raw_x11)]
-        blend(*steps[0])
-        candidate(*steps[1])
-        keep_state(*steps[1])
-        for a in range(PASSES):
-            x_q[a, 1] = quantize("x%d1" % a, x_round[a])
-        pending = []
-        for s, (t, h) in enumerate(steps):
-            if s + 1 < len(steps):
-                blend(*steps[s + 1])
-            if s + 2 < len(steps):
-                ahead = steps[s + 2]
-                if ahead not in z:
-                    gate(*ahead)
-                keep_state(*ahead)
-                candidate(*ahead)
-            scatter(t, h)
-            for job in pending[:3]:
-                round_y(nc.scalar.copy, *job)
-            pending = pending[3:]
-            if h == HALVES - 1:
-                nc.sync.dma_start(out_dealt[t], pages[t][:])
-                if t < PACK - 1:
-                    pending = pending + [(t, c) for c in range(CHUNKS)]
-        for job in pending:
-            round_y(nc.scalar.copy, *job)
+        x_q[0, 1] = quantize("x01", round_x(raw_x01, [(on_scalar, 0, 192), (on_vector, 192, HALF)]))
+        x_q[1, 1] = quantize("x11", round_x(raw_x11, [(on_scalar, 0, 192), (on_vector, 192, HALF)]))
+        for t in range(PACK):
+            gate(t, 1)
+        for t in range(1):
+            keep_state(t, both)
+        wn_q[0] = quantize("wn0", round_w(raw_wn0, [(on_scalar, 0, 2), (on_scalar, 2, 4)]))
+        wn_q[1] = quantize("wn1", round_w(raw_wn1, [(on_scalar, 0, 2), (on_scalar, 2, 4)]))
+        for t in range(PACK):
+            for h in both:
+                if (t, h) in on_vector_alone:
+                    first_candidate(t, h)
+                else:
+                    candidate(t, h)
+            if 1 + t < PACK:
+                keep_state(1 + t, both)
+        for s, (t, halves) in enumerate(steps):
+            gate_candidate(t, [h for h in halves if (t, h) not in on_vector_alone])
+            mix(t, halves)
+            scatter(t, halves)
+            nc.sync.dma_start(out_dealt[t], pages[t][:])
+        for t in range(PACK - 1):
+            for c in range(CHUNKS):
+                round_y(nc.scalar.copy, t, c)
 
         last = PACK - 1
         words_out = as_words(out_1)
@@ -265,7 +295,7 @@ def tile_list_tgn_mguP_kernel(
             nc.vector.quantize_mx(
                 out=y_codes[:, cols].bitcast(FP8X4),
                 scales=y_plane[:, cols],
-                in_=y_rounded[c][:].rearrange("p c i -> p (c i)"),
+                in_=scratch[c][:].bitcast(BF16),
             )
             nc.sync.dma_start(words_out[:, cols], y_codes[:, cols].bitcast(I32))
         for q in range(4):

@@ -20,11 +20,16 @@ P = 128
 PACK = 4
 K_PASS = P * PACK
 PASSES = K // K_PASS
+QUADRANT = 32
+SCALE_ROWS = 4
 HALF = 512
 HALVES = J // HALF
+BLOCKS = HALF // P
 LIST_COLS = HALF // 16
 CHUNK = 512
 CHUNKS = T // CHUNK
+STAGED = 8
+X_ON_SCALAR = 192
 
 
 def tile_list_tgn_mguP_kernel(
@@ -32,19 +37,24 @@ def tile_list_tgn_mguP_kernel(
     out_0, out_1, out_2,
 ):
     nc = tc.nc
+    on_scalar, on_vector = nc.scalar.copy, nc.vector.tensor_copy
     with ExitStack() as ctx:
         keep = ctx.enter_context(tc.tile_pool(name="keep", bufs=1))
-        stage = ctx.enter_context(tc.tile_pool(name="stage", bufs=8))
+        stage = ctx.enter_context(tc.tile_pool(name="stage", bufs=STAGED))
         rounded = ctx.enter_context(tc.tile_pool(name="rounded", bufs=3))
-        gates = ctx.enter_context(tc.tile_pool(name="gates", bufs=4))
-        work = ctx.enter_context(tc.tile_pool(name="work", bufs=2))
         psum = ctx.enter_context(tc.psum_pool(name="psum", bufs=1))
+
+        def as_words(packed):
+            return packed[0].rearrange("p c i -> p (c i)").bitcast(I32)
+
+        def half_cols(h):
+            return slice(h * HALF, (h + 1) * HALF)
+
+        def blocks(h):
+            return [(slice(b * P, (b + 1) * P), slice(h * HALF + b * P, h * HALF + (b + 1) * P)) for b in range(BLOCKS)]
 
         offsets = keep.tile([P, J // 16], U16, name="offsets")
         nc.sync.dma_start(offsets[:], offs)
-
-        def as_words(ap):
-            return ap[0].rearrange("p c i -> p (c i)").bitcast(I32)
 
         def zeroed_plane(name, width):
             plane = keep.tile([P, width], U8, name=name, align_bytes=64)
@@ -52,27 +62,54 @@ def tile_list_tgn_mguP_kernel(
             return plane
 
         def load_scale_rows(plane, first, scales):
-            for q in range(4):
-                rows = slice(32 * q + first, 32 * q + first + 4)
-                nc.sync.dma_start(plane[rows, :].bitcast(I32), scales[0, 4 * q : 4 * q + 4, :].bitcast(I32))
+            for r in range(SCALE_ROWS):
+                nc.sync.dma_start(
+                    plane[first + r : P : QUADRANT, :].bitcast(I32), scales[0, r : 16 : SCALE_ROWS, :].bitcast(I32)
+                )
+
+        def load_rows(src, a, cols):
+            raw = stage.tile([P, PACK, HALF], F32, name="staged")
+            nc.sync.dma_start(raw[:], src[a * K_PASS : (a + 1) * K_PASS, cols].rearrange("(p i) c -> p i c", i=PACK))
+            return raw
+
+        def load_state(t):
+            state = stage.tile([P, T], F32, name="staged")
+            nc.sync.dma_start(state[:], hT.rearrange("(p t) c -> t p c", t=PACK)[t])
+            return state
 
         tab_plane = zeroed_plane("tab_plane", T)
         u_plane = zeroed_plane("u_plane", N)
         bias_z = keep.tile([P, PACK], F32, name="bias_z")
         bias_n = keep.tile([P, PACK], F32, name="bias_n")
-        tab = stage.tile([P, T], I32, name="raw")
+        tab = stage.tile([P, T], I32, name="staged")
         uz_raw = keep.tile([P, N], I32, name="uz_raw")
         un_raw = keep.tile([P, N], I32, name="un_raw")
         nc.sync.dma_start(tab[:], as_words(tab_words))
 
         pages = [keep.tile([P, T], F32, name="page%d" % t) for t in range(PACK)]
-        for t in range(PACK):
-            nc.gpsimd.memset(pages[t][:], 0.0)
+        nc.vector.memset(pages[0][:], 0.0)
+        for page in pages[1:]:
+            nc.gpsimd.memset(page[:], 0.0)
+        weights = keep.tile([P, J], F32, name="weights")
+        identity = keep.tile([P, P], F32, name="identity")
+        make_identity(nc, identity[:])
 
-        def load_rows(src, a, cols):
-            raw = stage.tile([P, PACK, HALF], F32, name="raw")
-            nc.sync.dma_start(raw[:], src[a * K_PASS : (a + 1) * K_PASS, cols].rearrange("(p i) c -> p i c", i=PACK))
-            return raw
+        all_n = slice(0, N)
+        load_scale_rows(tab_plane, 0, tab_scales)
+        raw_wz0 = load_rows(wz, 0, all_n)
+        raw_x00 = load_rows(x, 0, half_cols(0))
+        nc.sync.dma_start(uz_raw[:], as_words(uz_words))
+        load_scale_rows(u_plane, 0, uz_scales)
+        raw_wz1 = load_rows(wz, 1, all_n)
+        nc.sync.dma_start(un_raw[:], as_words(un_words))
+        raw_x10 = load_rows(x, 1, half_cols(0))
+        load_scale_rows(u_plane, SCALE_ROWS, un_scales)
+        nc.sync.dma_start(bias_z[:], bz.rearrange("(p t) -> p t", t=PACK))
+        raw_x1 = [load_rows(x, a, half_cols(1)) for a in range(PASSES)]
+        raw_wn = [load_rows(wn, a, all_n) for a in range(PASSES)]
+        nc.sync.dma_start(bias_n[:], bn.rearrange("(p t) -> p t", t=PACK))
+        nc.sync.dma_start(weights[:], wgo)
+        states = [load_state(t) for t in range(PACK)]
 
         def round_x(raw, parts):
             grouped = rounded.tile([P, HALF * PACK], BF16, name="grouped", align_bytes=64)
@@ -96,7 +133,7 @@ def tile_list_tgn_mguP_kernel(
             codes = keep.tile([P, HALF], U32, name=name + "_codes", align_bytes=64)
             plane = keep.tile([P, HALF], U8, name=name + "_plane", align_bytes=64)
             nc.vector.quantize_mx(out=codes[:].bitcast(FP8X4), scales=plane[:], in_=grouped)
-            return codes, plane
+            return codes[:], plane[:]
 
         def deal_packed(name, raw, dtype):
             dealt = keep.tile([P, N], dtype, name=name, align_bytes=64)
@@ -105,61 +142,23 @@ def tile_list_tgn_mguP_kernel(
             )
             return dealt
 
-        states = [None] * PACK
-        weights = keep.tile([P, J], F32, name="weights")
-        hT_dealt = hT.rearrange("(p t) c -> t p c", t=PACK)
-        out_dealt = out_0.rearrange("(p t) c -> t p c", t=PACK)
-        identity = keep.tile([P, P], F32, name="identity")
-        make_identity(nc, identity[:])
-
-        def load_state(t):
-            states[t] = stage.tile([P, T], F32, name="raw")
-            nc.sync.dma_start(states[t][:], hT_dealt[t])
-
-        def half_cols(h):
-            return slice(h * HALF, (h + 1) * HALF)
-
-        every = slice(0, N)
-        load_scale_rows(tab_plane, 0, tab_scales)
-        raw_wz0 = load_rows(wz, 0, every)
-        raw_x00 = load_rows(x, 0, half_cols(0))
-        nc.sync.dma_start(uz_raw[:], as_words(uz_words))
-        load_scale_rows(u_plane, 0, uz_scales)
-        raw_wz1 = load_rows(wz, 1, every)
-        nc.sync.dma_start(un_raw[:], as_words(un_words))
-        raw_x10 = load_rows(x, 1, half_cols(0))
-        load_scale_rows(u_plane, 4, un_scales)
-        nc.sync.dma_start(bias_z[:], bz.rearrange("(p t) -> p t", t=PACK))
-        raw_x01 = load_rows(x, 0, half_cols(1))
-        raw_x11 = load_rows(x, 1, half_cols(1))
-        raw_wn0 = load_rows(wn, 0, every)
-        load_state(0)
-        raw_wn1 = load_rows(wn, 1, every)
-        nc.sync.dma_start(bias_n[:], bn.rearrange("(p t) -> p t", t=PACK))
-        load_state(1)
-        nc.sync.dma_start(weights[:, half_cols(0)], wgo[:, half_cols(0)])
-        nc.sync.dma_start(weights[:, half_cols(1)], wgo[:, half_cols(1)])
-        load_state(2)
-        load_state(3)
-
-        on_scalar, on_vector = nc.scalar.copy, nc.vector.tensor_copy
         v_codes = keep.tile([P, J], U32, name="v_codes", align_bytes=64)
         v_plane = keep.tile([P, J], U8, name="v_plane", align_bytes=64)
         nc.vector.tensor_copy(v_codes[:], tab[:].bitcast(U32).indirect(offsets[:]))
         nc.vector.tensor_copy(v_plane[:], tab_plane[:].indirect(offsets[:]))
 
-        wz_q = [None] * PASSES
-        wn_q = [None] * PASSES
+        x_shared = [(on_scalar, 0, X_ON_SCALAR), (on_vector, X_ON_SCALAR, HALF)]
+        w_shared = [(on_scalar, 0, PACK // 2), (on_vector, PACK // 2, PACK)]
         x_q = {}
-        wz_q[0] = quantize("wz0", round_w(raw_wz0, [(on_scalar, 0, 4)]))
+        wz0_q = quantize("wz0", round_w(raw_wz0, [(on_scalar, 0, PACK)]))
         x_q[0, 0] = quantize("x00", round_x(raw_x00, [(on_scalar, 0, HALF)]))
         uz_codes = deal_packed("uz_codes", uz_raw, I32)
         un_codes = deal_packed("un_codes", un_raw, I32)
         u_dealt = deal_packed("u_dealt", u_plane, U8)
-        uz_q = uz_codes, u_dealt[:]
-        un_q = un_codes, u_dealt[4:P, :]
-        wz_q[1] = quantize("wz1", round_w(raw_wz1, [(on_scalar, 0, 2), (on_vector, 2, 4)]))
-        x_q[1, 0] = quantize("x10", round_x(raw_x10, [(on_scalar, 0, 192), (on_vector, 192, HALF)]))
+        uz_q = uz_codes[:], u_dealt[:]
+        un_q = un_codes[:], u_dealt[SCALE_ROWS:P, :]
+        wz_q = [wz0_q, quantize("wz1", round_w(raw_wz1, w_shared))]
+        x_q[1, 0] = quantize("x10", round_x(raw_x10, x_shared))
 
         def product(acc, t, terms):
             rows = slice(t * P, (t + 1) * P)
@@ -174,129 +173,150 @@ def tile_list_tgn_mguP_kernel(
                     stop=(n == len(terms) - 1),
                 )
 
-        def x_term(w_q, a, h):
-            return w_q[a], (x_q[a, h][0][:], x_q[a, h][1][:])
+        def x_terms(w_q, h):
+            return [(w_q[a], x_q[a, h]) for a in range(PASSES)]
 
         def v_term(u_q, h):
             return u_q, (v_codes[:, half_cols(h)], v_plane[:, half_cols(h)])
 
-        z = [gates.tile([P, J], F32, name="z") for t in range(PACK)]
-        zhn = [gates.tile([P, J], F32, name="zhn") for t in range(PACK)]
-        scratch = [keep.tile([P, CHUNK * PACK // 2], F32, name="scratch%d" % c, align_bytes=64) for c in range(CHUNKS)]
-        kept = {}
+        def add_turned(acc, first, second):
+            nc.tensor.matmul(acc, first, identity[:], is_transpose=True, start=True, stop=False)
+            nc.tensor.matmul(acc, second, identity[:], is_transpose=True, start=False, stop=True)
 
-        def span(halves):
-            return slice(halves[0] * HALF, (halves[-1] + 1) * HALF)
+        def sum_bank():
+            return psum.tile([P, HALF], F32, name="sum_bank", bufs=3)
 
-        def listed(halves):
-            return offsets[:, halves[0] * LIST_COLS : (halves[-1] + 1) * LIST_COLS]
+        def inner_bank():
+            return psum.tile([P, HALF], F32, name="inner_bank", bufs=2)
+
+        def difference_bank():
+            return psum.tile([P, HALF], F32, name="difference_bank", bufs=2)
+
+        def turn_bank():
+            return psum.tile([P, HALF], F32, name="turn_bank", bufs=1)
+
+        z = [keep.tile([P, J], F32, name="z%d" % t, align_bytes=64) for t in range(PACK)]
+        running = [keep.tile([P, J], F32, name="running%d" % t) for t in range(PACK)]
+        kept = [keep.tile([P, J], F32, name="kept%d" % t) for t in range(PACK)]
+        by_event = keep.tile([P, HALVES * BLOCKS], F32, name="by_event")
+        scratch = [keep.tile([P, PACK * CHUNK // 2], F32, name="scratch%d" % b, align_bytes=64) for b in range(BLOCKS)]
+
+        def operand_blocks(t, h):
+            first = (HALVES * t + h) % PACK * (CHUNK // 2)
+            return [scratch[b][:, first : first + P] for b in range(BLOCKS)]
 
         def gate(t, h):
-            sz = psum.tile([P, HALF], F32, name="sz", tag="a", bufs=3)
-            hn = psum.tile([P, HALF], F32, name="hn", tag="b", bufs=2)
-            product(sz, t, [v_term(uz_q, h)] + [x_term(wz_q, a, h) for a in range(PASSES)])
+            sz = sum_bank()
+            hn = inner_bank()
+            product(sz, t, [v_term(uz_q, h)] + x_terms(wz_q, h))
             product(hn, t, [v_term(un_q, h)])
             nc.scalar.activation(z[t][:, half_cols(h)], sz[:], ACT.Sigmoid, bias=bias_z[:, t : t + 1])
-            nc.vector.tensor_tensor(zhn[t][:, half_cols(h)], hn[:], z[t][:, half_cols(h)], ALU.mult)
+            nc.vector.tensor_tensor(running[t][:, half_cols(h)], hn[:], z[t][:, half_cols(h)], ALU.mult)
 
-        def keep_state(t, halves):
-            width = HALF * len(halves)
-            rest = work.tile([P, width], F32, name="rest", bufs=2)
-            kept[t, halves] = work.tile([P, width], F32, name="kept", bufs=4)
-            nc.scalar.activation(rest[:], z[t][:, span(halves)], ACT.Identity, bias=1.0, scale=-1.0)
-            nc.vector.tensor_tensor(kept[t, halves][:], states[t][:].indirect(listed(halves)), rest[:], ALU.mult)
+        def turn_weights(h):
+            turned = turn_bank()
+            for block, events in blocks(h):
+                nc.tensor.transpose(turned[:, block], weights[:, events], identity[:])
+            nc.scalar.copy(by_event[:, h * BLOCKS : (h + 1) * BLOCKS], turned[:, 0:HALF:P])
+
+        def gather_state(t):
+            nc.vector.tensor_tensor(kept[t][:], states[t][:].indirect(offsets[:]), weights[:], ALU.mult)
 
         def candidate(t, h):
-            xn = psum.tile([P, HALF], F32, name="xn", tag="a", bufs=3)
-            product(xn, t, [x_term(wn_q, a, h) for a in range(PASSES)])
-            biased = [scratch[b][:, h * P : (h + 1) * P] for b in range(HALF // P)]
-            for b in range(HALF // P):
-                nc.scalar.activation(biased[b], xn[:, b * P : (b + 1) * P], ACT.Identity, bias=bias_n[:, t : t + 1])
-            pre = psum.tile([P, HALF], F32, name="pre", tag="b", bufs=2)
-            for b in range(HALF // P):
-                block = slice(b * P, (b + 1) * P)
-                events = slice(h * HALF + b * P, h * HALF + (b + 1) * P)
-                nc.tensor.matmul(pre[:, block], biased[b], identity[:], is_transpose=True, start=True, stop=False)
-                nc.tensor.matmul(pre[:, block], zhn[t][:, events], identity[:], is_transpose=True, start=False, stop=True)
-            nc.scalar.activation(zhn[t][:, half_cols(h)], pre[:], ACT.Tanh)
+            xn = sum_bank()
+            product(xn, t, x_terms(wn_q, h))
+            operands = operand_blocks(t, h)
+            for b, (block, events) in enumerate(blocks(h)):
+                nc.scalar.activation(operands[b], xn[:, block], ACT.Identity, bias=bias_n[:, t : t + 1])
+            argument = inner_bank()
+            for b, (block, events) in enumerate(blocks(h)):
+                add_turned(argument[:, block], operands[b], running[t][:, events])
+            nc.scalar.activation(running[t][:, half_cols(h)], argument[:], ACT.Tanh)
+            turned = turn_bank()
+            for block, events in blocks(h):
+                nc.tensor.transpose(turned[:, block], kept[t][:, events], identity[:])
+            for b, (block, events) in enumerate(blocks(h)):
+                nc.scalar.activation(operands[b], turned[:, block], ACT.Copy, scale=-1.0)
+            for b, (block, events) in enumerate(blocks(h)):
+                c = h * BLOCKS + b
+                part = running[t][:, events]
+                nc.scalar.activation(part, part, ACT.Copy, scale=by_event[:, c : c + 1])
 
-        def first_candidate(t, h):
-            xn = psum.tile([P, HALF], F32, name="xn", tag="a", bufs=3)
-            product(xn, t, [x_term(wn_q, a, h) for a in range(PASSES)])
-            part = zhn[t][:, half_cols(h)]
-            nc.vector.tensor_tensor(part, xn[:], part, ALU.add)
-            nc.scalar.activation(part, part, ACT.Tanh, bias=bias_n[:, t : t + 1])
-            nc.vector.tensor_tensor(part, part, z[t][:, half_cols(h)], ALU.mult)
+        def gated_difference(t, h):
+            difference = difference_bank()
+            for b, (block, events) in enumerate(blocks(h)):
+                add_turned(difference[:, block], running[t][:, events], operand_blocks(t, h)[b])
+            nc.vector.tensor_tensor(running[t][:, half_cols(h)], difference[:], z[t][:, half_cols(h)], ALU.mult)
 
-        def gate_candidate(t, halves):
-            for h in halves:
-                cand = psum.tile([P, HALF], F32, name="cand", tag="c", bufs=3)
-                for b in range(HALF // P):
-                    events = slice(h * HALF + b * P, h * HALF + (b + 1) * P)
-                    nc.tensor.transpose(cand[:, b * P : (b + 1) * P], zhn[t][:, events], identity[:])
-                nc.vector.tensor_tensor(zhn[t][:, half_cols(h)], cand[:], z[t][:, half_cols(h)], ALU.mult)
+        def scatter(t, first, stop):
+            events = slice(first * HALF, stop * HALF)
+            listed = offsets[:, first * LIST_COLS : stop * LIST_COLS]
+            nc.vector.tensor_tensor(pages[t][:].indirect(listed), running[t][:, events], kept[t][:, events], ALU.add)
 
-        def mix(t, halves):
-            part = zhn[t][:, span(halves)]
-            nc.vector.tensor_tensor(part, part, kept[t, halves][:], ALU.add)
-
-        def scatter(t, halves):
-            nc.vector.tensor_tensor(
-                pages[t][:].indirect(listed(halves)), zhn[t][:, span(halves)], weights[:, span(halves)], ALU.mult
-            )
-
-        y_rounded = [scratch[c][:].bitcast(BF16).rearrange("p (c i) -> p c i", i=PACK) for c in range(CHUNKS)]
-        y_codes = keep.tile([P, T], U32, name="y_codes", align_bytes=64)
-        y_plane = keep.tile([P, T], U8, name="y_plane", align_bytes=64)
-        upper = [keep.tile([P, 2, CHUNK], BF16, name="upper%d" % c) for c in range(CHUNKS // 2)]
-
-        def round_y(copy, t, c):
-            by_rows = t >= 2 and c < CHUNKS // 2
-            copy(upper[c][:, t - 2, :] if by_rows else y_rounded[c][:, :, t], pages[t][:, c * CHUNK : (c + 1) * CHUNK])
-
-        both = (0, 1)
-        steps = [(t, both) for t in range(PACK)]
-        on_vector_alone = ((0, 0), (0, 1))
         for t in range(PACK):
             gate(t, 0)
-        x_q[0, 1] = quantize("x01", round_x(raw_x01, [(on_scalar, 0, 192), (on_vector, 192, HALF)]))
-        x_q[1, 1] = quantize("x11", round_x(raw_x11, [(on_scalar, 0, 192), (on_vector, 192, HALF)]))
+        for a in range(PASSES):
+            x_q[a, 1] = quantize("x%d1" % a, round_x(raw_x1[a], x_shared))
         for t in range(PACK):
             gate(t, 1)
-        for t in range(1):
-            keep_state(t, both)
-        wn_q[0] = quantize("wn0", round_w(raw_wn0, [(on_scalar, 0, 2), (on_scalar, 2, 4)]))
-        wn_q[1] = quantize("wn1", round_w(raw_wn1, [(on_scalar, 0, 2), (on_scalar, 2, 4)]))
-        for t in range(PACK):
-            for h in both:
-                if (t, h) in on_vector_alone:
-                    first_candidate(t, h)
-                else:
-                    candidate(t, h)
-            if 1 + t < PACK:
-                keep_state(1 + t, both)
-        for s, (t, halves) in enumerate(steps):
-            gate_candidate(t, [h for h in halves if (t, h) not in on_vector_alone])
-            mix(t, halves)
-            scatter(t, halves)
-            nc.sync.dma_start(out_dealt[t], pages[t][:])
-        for t in range(PACK - 1):
-            for c in range(CHUNKS):
-                round_y(nc.scalar.copy, t, c)
+        for h in range(HALVES):
+            turn_weights(h)
+        gather_state(0)
+        wn_q = [quantize("wn%d" % a, round_w(raw_wn[a], w_shared)) for a in range(PASSES)]
+        for t in range(1, PACK):
+            gather_state(t)
 
+        tiles = [(t, h) for t in range(PACK) for h in range(HALVES)]
+        for t, h in tiles[:PACK]:
+            candidate(t, h)
+        for n, (t, h) in enumerate(tiles):
+            gated_difference(t, h)
+            if n + PACK < len(tiles):
+                candidate(*tiles[n + PACK])
+            if t == 0:
+                scatter(t, h, h + 1)
+            elif h == HALVES - 1:
+                scatter(t, 0, HALVES)
+            if h == HALVES - 1:
+                nc.sync.dma_start(out_0.rearrange("(p t) c -> t p c", t=PACK)[t], pages[t][:])
+
+        y_rows = [scratch[c][:].bitcast(BF16).rearrange("p (t c) -> p t c", t=PACK) for c in range(CHUNKS)]
+        y_woven = [z[c][:].bitcast(BF16).rearrange("p (c t) -> p c t", t=PACK) for c in range(CHUNKS)]
+        y_codes = keep.tile([P, T], U32, name="y_codes", align_bytes=64)
+        y_plane = keep.tile([P, T], U8, name="y_plane", align_bytes=64)
+        vector_chunks = range(CHUNKS // 2)
+        scalar_chunks = range(CHUNKS // 2, CHUNKS)
         last = PACK - 1
-        words_out = as_words(out_1)
+
+        def chunk_cols(c):
+            return slice(c * CHUNK, (c + 1) * CHUNK)
+
+        def weave(copy, c, first, stop):
+            copy(y_woven[c][:, :, first:stop], y_rows[c][:, first:stop, :].rearrange("p t c -> p c t"))
+
+        def round_slice(t):
+            for c in range(CHUNKS):
+                on_scalar(y_rows[c][:, t, :], pages[t][:, chunk_cols(c)])
+
+        round_slice(0)
+        round_slice(1)
+        for c in vector_chunks:
+            weave(on_scalar, c, 0, 2)
+        round_slice(2)
+        for c in scalar_chunks:
+            weave(on_scalar, c, 0, last)
+        for c in vector_chunks:
+            on_vector(y_rows[c][:, last, :], pages[last][:, chunk_cols(c)])
+        for c in vector_chunks:
+            weave(on_vector, c, 2, PACK)
+        for c in scalar_chunks:
+            on_scalar(y_woven[c][:, :, last], pages[last][:, chunk_cols(c)])
         for c in range(CHUNKS):
-            round_y(nc.vector.tensor_copy if c < CHUNKS // 2 else nc.scalar.copy, last, c)
-        for c in range(CHUNKS // 2):
-            nc.vector.tensor_copy(y_rounded[c][:, :, 2:4], upper[c][:].rearrange("p i c -> p c i"))
-        for c in range(CHUNKS):
-            cols = slice(c * CHUNK, (c + 1) * CHUNK)
             nc.vector.quantize_mx(
-                out=y_codes[:, cols].bitcast(FP8X4),
-                scales=y_plane[:, cols],
-                in_=scratch[c][:].bitcast(BF16),
+                out=y_codes[:, chunk_cols(c)].bitcast(FP8X4),
+                scales=y_plane[:, chunk_cols(c)],
+                in_=z[c][:].bitcast(BF16),
             )
-            nc.sync.dma_start(words_out[:, cols], y_codes[:, cols].bitcast(I32))
-        for q in range(4):
-            nc.scalar.dma_start(out_2[0, 4 * q : 4 * q + 4, :].bitcast(I32), y_plane[32 * q : 32 * q + 4, :].bitcast(I32))
+            nc.sync.dma_start(as_words(out_1)[:, chunk_cols(c)], y_codes[:, chunk_cols(c)].bitcast(I32))
+        for r in range(SCALE_ROWS):
+            nc.scalar.dma_start(out_2[0, r : 16 : SCALE_ROWS, :].bitcast(I32), y_plane[r:P:QUADRANT, :].bitcast(I32))

from contextlib import ExitStack

import concourse.mybir as mybir
from concourse.masks import make_identity

K, M, N, T, J = 1024, 512, 512, 2048, 1024
FLOPS = 2 * J * N * (2 * K + 2 * M)

F32 = mybir.dt.float32
BF16 = mybir.dt.bfloat16
I32 = mybir.dt.int32
U32 = mybir.dt.uint32
U16 = mybir.dt.uint16
U8 = mybir.dt.uint8
FP8X4 = mybir.dt.float8_e4m3fn_x4
ACT = mybir.ActivationFunctionType
ALU = mybir.AluOpType

P = 128
PACK = 4
K_PASS = P * PACK
PASSES = K // K_PASS
QUADRANT = 32
SCALE_ROWS = 4
HALF = 512
HALVES = J // HALF
BLOCKS = HALF // P
LIST_COLS = HALF // 16
CHUNK = 512
CHUNKS = T // CHUNK
STAGED = 8
X_ON_SCALAR = 192


def tile_list_tgn_mguP_kernel(
    tc, x, tab_words, tab_scales, wz, uz_words, uz_scales, wn, un_words, un_scales, bz, bn, hT, wgo, offs,
    out_0, out_1, out_2,
):
    nc = tc.nc
    on_scalar, on_vector = nc.scalar.copy, nc.vector.tensor_copy
    with ExitStack() as ctx:
        keep = ctx.enter_context(tc.tile_pool(name="keep", bufs=1))
        stage = ctx.enter_context(tc.tile_pool(name="stage", bufs=STAGED))
        rounded = ctx.enter_context(tc.tile_pool(name="rounded", bufs=3))
        psum = ctx.enter_context(tc.psum_pool(name="psum", bufs=1))

        def as_words(packed):
            return packed[0].rearrange("p c i -> p (c i)").bitcast(I32)

        def half_cols(h):
            return slice(h * HALF, (h + 1) * HALF)

        def blocks(h):
            return [(slice(b * P, (b + 1) * P), slice(h * HALF + b * P, h * HALF + (b + 1) * P)) for b in range(BLOCKS)]

        offsets = keep.tile([P, J // 16], U16, name="offsets")
        nc.sync.dma_start(offsets[:], offs)

        def zeroed_plane(name, width):
            plane = keep.tile([P, width], U8, name=name, align_bytes=64)
            nc.gpsimd.memset(plane[:].bitcast(I32), 0)
            return plane

        def load_scale_rows(plane, first, scales):
            for r in range(SCALE_ROWS):
                nc.sync.dma_start(
                    plane[first + r : P : QUADRANT, :].bitcast(I32), scales[0, r : 16 : SCALE_ROWS, :].bitcast(I32)
                )

        def load_rows(src, a, cols):
            raw = stage.tile([P, PACK, HALF], F32, name="staged")
            nc.sync.dma_start(raw[:], src[a * K_PASS : (a + 1) * K_PASS, cols].rearrange("(p i) c -> p i c", i=PACK))
            return raw

        def load_state(t):
            state = stage.tile([P, T], F32, name="staged")
            nc.sync.dma_start(state[:], hT.rearrange("(p t) c -> t p c", t=PACK)[t])
            return state

        tab_plane = zeroed_plane("tab_plane", T)
        u_plane = zeroed_plane("u_plane", N)
        bias_z = keep.tile([P, PACK], F32, name="bias_z")
        bias_n = keep.tile([P, PACK], F32, name="bias_n")
        tab = stage.tile([P, T], I32, name="staged")
        uz_raw = keep.tile([P, N], I32, name="uz_raw")
        un_raw = keep.tile([P, N], I32, name="un_raw")
        nc.sync.dma_start(tab[:], as_words(tab_words))

        pages = [keep.tile([P, T], F32, name="page%d" % t) for t in range(PACK)]
        nc.vector.memset(pages[0][:], 0.0)
        for page in pages[1:]:
            nc.gpsimd.memset(page[:], 0.0)
        weights = keep.tile([P, J], F32, name="weights")
        identity = keep.tile([P, P], F32, name="identity")
        make_identity(nc, identity[:])

        all_n = slice(0, N)
        load_scale_rows(tab_plane, 0, tab_scales)
        raw_wz0 = load_rows(wz, 0, all_n)
        raw_x00 = load_rows(x, 0, half_cols(0))
        nc.sync.dma_start(uz_raw[:], as_words(uz_words))
        load_scale_rows(u_plane, 0, uz_scales)
        raw_wz1 = load_rows(wz, 1, all_n)
        nc.sync.dma_start(un_raw[:], as_words(un_words))
        raw_x10 = load_rows(x, 1, half_cols(0))
        load_scale_rows(u_plane, SCALE_ROWS, un_scales)
        nc.sync.dma_start(bias_z[:], bz.rearrange("(p t) -> p t", t=PACK))
        raw_x1 = [load_rows(x, a, half_cols(1)) for a in range(PASSES)]
        raw_wn = [load_rows(wn, a, all_n) for a in range(PASSES)]
        nc.sync.dma_start(bias_n[:], bn.rearrange("(p t) -> p t", t=PACK))
        nc.sync.dma_start(weights[:], wgo)
        states = [load_state(t) for t in range(PACK)]

        def round_x(raw, parts):
            grouped = rounded.tile([P, HALF * PACK], BF16, name="grouped", align_bytes=64)
            for copy, first, stop in parts:
                copy(
                    grouped[:, first * PACK : stop * PACK].rearrange("p (c e i) -> p c i e", e=4, i=PACK),
                    raw[:, :, first:stop].rearrange("p i (c e) -> p c i e", e=4),
                )
            return grouped[:]

        def round_w(raw, parts):
            grouped = rounded.tile([P, PACK, P * PACK], BF16, name="grouped", align_bytes=64)
            for copy, first, stop in parts:
                copy(
                    grouped[:, first:stop, :].rearrange("p t (m i) -> p m i t", i=PACK),
                    raw[:].rearrange("p i (m t) -> p m i t", t=PACK)[:, :, :, first:stop],
                )
            return grouped[:].rearrange("p t c -> p (t c)")

        def quantize(name, grouped):
            codes = keep.tile([P, HALF], U32, name=name + "_codes", align_bytes=64)
            plane = keep.tile([P, HALF], U8, name=name + "_plane", align_bytes=64)
            nc.vector.quantize_mx(out=codes[:].bitcast(FP8X4), scales=plane[:], in_=grouped)
            return codes[:], plane[:]

        def deal_packed(name, raw, dtype):
            dealt = keep.tile([P, N], dtype, name=name, align_bytes=64)
            nc.vector.tensor_copy(
                dealt[:].rearrange("p (t m) -> p m t", t=PACK), raw[:].rearrange("p (m t) -> p m t", t=PACK)
            )
            return dealt

        v_codes = keep.tile([P, J], U32, name="v_codes", align_bytes=64)
        v_plane = keep.tile([P, J], U8, name="v_plane", align_bytes=64)
        nc.vector.tensor_copy(v_codes[:], tab[:].bitcast(U32).indirect(offsets[:]))
        nc.vector.tensor_copy(v_plane[:], tab_plane[:].indirect(offsets[:]))

        x_shared = [(on_scalar, 0, X_ON_SCALAR), (on_vector, X_ON_SCALAR, HALF)]
        w_shared = [(on_scalar, 0, PACK // 2), (on_vector, PACK // 2, PACK)]
        x_q = {}
        wz0_q = quantize("wz0", round_w(raw_wz0, [(on_scalar, 0, PACK)]))
        x_q[0, 0] = quantize("x00", round_x(raw_x00, [(on_scalar, 0, HALF)]))
        uz_codes = deal_packed("uz_codes", uz_raw, I32)
        un_codes = deal_packed("un_codes", un_raw, I32)
        u_dealt = deal_packed("u_dealt", u_plane, U8)
        uz_q = uz_codes[:], u_dealt[:]
        un_q = un_codes[:], u_dealt[SCALE_ROWS:P, :]
        wz_q = [wz0_q, quantize("wz1", round_w(raw_wz1, w_shared))]
        x_q[1, 0] = quantize("x10", round_x(raw_x10, x_shared))

        def product(acc, t, terms):
            rows = slice(t * P, (t + 1) * P)
            for n, (stationary, moving) in enumerate(terms):
                nc.tensor.matmul_mx(
                    out=acc[:],
                    lhsT=stationary[0][:, rows].bitcast(FP8X4),
                    lhsT_scale=stationary[1][:, rows],
                    rhs=moving[0].bitcast(FP8X4),
                    rhs_scale=moving[1],
                    start=(n == 0),
                    stop=(n == len(terms) - 1),
                )

        def x_terms(w_q, h):
            return [(w_q[a], x_q[a, h]) for a in range(PASSES)]

        def v_term(u_q, h):
            return u_q, (v_codes[:, half_cols(h)], v_plane[:, half_cols(h)])

        def add_turned(acc, first, second):
            nc.tensor.matmul(acc, first, identity[:], is_transpose=True, start=True, stop=False)
            nc.tensor.matmul(acc, second, identity[:], is_transpose=True, start=False, stop=True)

        def sum_bank():
            return psum.tile([P, HALF], F32, name="sum_bank", bufs=3)

        def inner_bank():
            return psum.tile([P, HALF], F32, name="inner_bank", bufs=2)

        def difference_bank():
            return psum.tile([P, HALF], F32, name="difference_bank", bufs=2)

        def turn_bank():
            return psum.tile([P, HALF], F32, name="turn_bank", bufs=1)

        z = [keep.tile([P, J], F32, name="z%d" % t, align_bytes=64) for t in range(PACK)]
        running = [keep.tile([P, J], F32, name="running%d" % t) for t in range(PACK)]
        kept = [keep.tile([P, J], F32, name="kept%d" % t) for t in range(PACK)]
        by_event = keep.tile([P, HALVES * BLOCKS], F32, name="by_event")
        scratch = [keep.tile([P, PACK * CHUNK // 2], F32, name="scratch%d" % b, align_bytes=64) for b in range(BLOCKS)]

        def operand_blocks(t, h):
            first = (HALVES * t + h) % PACK * (CHUNK // 2)
            return [scratch[b][:, first : first + P] for b in range(BLOCKS)]

        def gate(t, h):
            sz = sum_bank()
            hn = inner_bank()
            product(sz, t, [v_term(uz_q, h)] + x_terms(wz_q, h))
            product(hn, t, [v_term(un_q, h)])
            nc.scalar.activation(z[t][:, half_cols(h)], sz[:], ACT.Sigmoid, bias=bias_z[:, t : t + 1])
            nc.vector.tensor_tensor(running[t][:, half_cols(h)], hn[:], z[t][:, half_cols(h)], ALU.mult)

        def turn_weights(h):
            turned = turn_bank()
            for block, events in blocks(h):
                nc.tensor.transpose(turned[:, block], weights[:, events], identity[:])
            nc.scalar.copy(by_event[:, h * BLOCKS : (h + 1) * BLOCKS], turned[:, 0:HALF:P])

        def gather_state(t):
            nc.vector.tensor_tensor(kept[t][:], states[t][:].indirect(offsets[:]), weights[:], ALU.mult)

        def candidate(t, h):
            xn = sum_bank()
            product(xn, t, x_terms(wn_q, h))
            operands = operand_blocks(t, h)
            for b, (block, events) in enumerate(blocks(h)):
                nc.scalar.activation(operands[b], xn[:, block], ACT.Identity, bias=bias_n[:, t : t + 1])
            argument = inner_bank()
            for b, (block, events) in enumerate(blocks(h)):
                add_turned(argument[:, block], operands[b], running[t][:, events])
            nc.scalar.activation(running[t][:, half_cols(h)], argument[:], ACT.Tanh)
            turned = turn_bank()
            for block, events in blocks(h):
                nc.tensor.transpose(turned[:, block], kept[t][:, events], identity[:])
            for b, (block, events) in enumerate(blocks(h)):
                nc.scalar.activation(operands[b], turned[:, block], ACT.Copy, scale=-1.0)
            for b, (block, events) in enumerate(blocks(h)):
                c = h * BLOCKS + b
                part = running[t][:, events]
                nc.scalar.activation(part, part, ACT.Copy, scale=by_event[:, c : c + 1])

        def gated_difference(t, h):
            difference = difference_bank()
            for b, (block, events) in enumerate(blocks(h)):
                add_turned(difference[:, block], running[t][:, events], operand_blocks(t, h)[b])
            nc.vector.tensor_tensor(running[t][:, half_cols(h)], difference[:], z[t][:, half_cols(h)], ALU.mult)

        def scatter(t, first, stop):
            events = slice(first * HALF, stop * HALF)
            listed = offsets[:, first * LIST_COLS : stop * LIST_COLS]
            nc.vector.tensor_tensor(pages[t][:].indirect(listed), running[t][:, events], kept[t][:, events], ALU.add)

        for t in range(PACK):
            gate(t, 0)
        for a in range(PASSES):
            x_q[a, 1] = quantize("x%d1" % a, round_x(raw_x1[a], x_shared))
        for t in range(PACK):
            gate(t, 1)
        for h in range(HALVES):
            turn_weights(h)
        gather_state(0)
        wn_q = [quantize("wn%d" % a, round_w(raw_wn[a], w_shared)) for a in range(PASSES)]
        for t in range(1, PACK):
            gather_state(t)

        tiles = [(t, h) for t in range(PACK) for h in range(HALVES)]
        for t, h in tiles[:PACK]:
            candidate(t, h)
        for n, (t, h) in enumerate(tiles):
            gated_difference(t, h)
            if n + PACK < len(tiles):
                candidate(*tiles[n + PACK])
            if t == 0:
                scatter(t, h, h + 1)
            elif h == HALVES - 1:
                scatter(t, 0, HALVES)
            if h == HALVES - 1:
                nc.sync.dma_start(out_0.rearrange("(p t) c -> t p c", t=PACK)[t], pages[t][:])

        y_rows = [scratch[c][:].bitcast(BF16).rearrange("p (t c) -> p t c", t=PACK) for c in range(CHUNKS)]
        y_woven = [z[c][:].bitcast(BF16).rearrange("p (c t) -> p c t", t=PACK) for c in range(CHUNKS)]
        y_codes = keep.tile([P, T], U32, name="y_codes", align_bytes=64)
        y_plane = keep.tile([P, T], U8, name="y_plane", align_bytes=64)
        vector_chunks = range(CHUNKS // 2)
        scalar_chunks = range(CHUNKS // 2, CHUNKS)
        last = PACK - 1

        def chunk_cols(c):
            return slice(c * CHUNK, (c + 1) * CHUNK)

        def weave(copy, c, first, stop):
            copy(y_woven[c][:, :, first:stop], y_rows[c][:, first:stop, :].rearrange("p t c -> p c t"))

        def round_slice(t):
            for c in range(CHUNKS):
                on_scalar(y_rows[c][:, t, :], pages[t][:, chunk_cols(c)])

        round_slice(0)
        round_slice(1)
        for c in vector_chunks:
            weave(on_scalar, c, 0, 2)
        round_slice(2)
        for c in scalar_chunks:
            weave(on_scalar, c, 0, last)
        for c in vector_chunks:
            on_vector(y_rows[c][:, last, :], pages[last][:, chunk_cols(c)])
        for c in vector_chunks:
            weave(on_vector, c, 2, PACK)
        for c in scalar_chunks:
            on_scalar(y_woven[c][:, :, last], pages[last][:, chunk_cols(c)])
        for c in range(CHUNKS):
            nc.vector.quantize_mx(
                out=y_codes[:, chunk_cols(c)].bitcast(FP8X4),
                scales=y_plane[:, chunk_cols(c)],
                in_=z[c][:].bitcast(BF16),
            )
            nc.sync.dma_start(as_words(out_1)[:, chunk_cols(c)], y_codes[:, chunk_cols(c)].bitcast(I32))
        for r in range(SCALE_ROWS):
            nc.scalar.dma_start(out_2[0, r : 16 : SCALE_ROWS, :].bitcast(I32), y_plane[r:P:QUADRANT, :].bitcast(I32))
